import numpy as np
import ml_dtypes


def mxq(x, axis, fmt="e4m3"):
    dtype, down = {"e4m3": (ml_dtypes.float8_e4m3fn, 7), "e5m2": (ml_dtypes.float8_e5m2, 14)}[fmt]
    v = np.moveaxis(np.asarray(x, np.float32).astype(ml_dtypes.bfloat16).astype(np.float64), axis, -1)
    blocks = v.reshape(v.shape[:-1] + (-1, 32))
    amax = np.abs(blocks).max(-1, keepdims=True)
    byte = np.maximum(np.where(amax > 0, np.frexp(amax)[1] - 1 + 127, 0) - down, 1)
    scale = np.exp2(byte - 127.0)
    codes = (blocks / scale).astype(np.float32).astype(dtype).astype(np.float64)
    return np.moveaxis((codes * scale).reshape(v.shape), -1, axis)


WIDE = False


def mx_kscale(k):
    if not WIDE:
        return np.ones(k)
    levels = np.array([10, -10, 5, -5, 0])
    if k % 512:
        return np.exp2(np.random.permutation(np.resize(levels, k // 32))).repeat(32)
    a = np.empty((k // 512, 16))
    for p in range(k // 512):
        a[p, :8] = np.random.permutation(np.resize(levels, 8))
        for g in range(8):
            far = levels[np.abs(levels - a[p, g]) >= 10]
            a[p, g + 8] = far[np.random.randint(len(far))]
    return np.exp2(a.ravel()).repeat(32)


def f64(x):
    return np.asarray(x).astype(np.float64)


def striped(idx):
    return np.tile(idx.reshape(-1, 16).T, (8, 1)).astype(np.uint16)


def unstriped(offs):
    return offs[:16].T.reshape(-1).astype(np.int64)


E2M1 = np.array([0.0, 0.5, 1.0, 1.5, 2.0, 3.0, 4.0, 6.0, -0.0, -0.5, -1.0, -1.5, -2.0, -3.0, -4.0, -6.0])


def pack_weight(w, fmt):
    k, n = w.shape
    w = f64(np.asarray(w, np.float32).astype(ml_dtypes.bfloat16)).reshape(k // 32, 32, n)
    amax = np.abs(w).max(1)
    if fmt == "e4m3":
        byte = np.frexp(amax)[1] - 1 + 127 - 7
    else:
        mant, ex = np.frexp(amax / 6.0)
        byte = np.where(mant > 0.5, ex, ex - 1) + 127
    byte = np.clip(np.where(amax > 0, byte, 1), 1, 254)
    scaled = (w * np.exp2(127.0 - byte)[:, None, :]).reshape(k, n).astype(np.float32)
    by_word = np.ascontiguousarray(scaled.reshape(k // 512, 128, 4, n).transpose(0, 1, 3, 2))
    if fmt == "e4m3":
        words = by_word.astype(ml_dtypes.float8_e4m3fn).view(np.uint8)
    else:
        c = by_word.astype(ml_dtypes.float4_e2m1fn).view(np.uint8) & 0xF
        words = (c[..., 0::2] | (c[..., 1::2] << 4)).reshape(k // 512, 128, 2 * n)
    return np.ascontiguousarray(words), np.ascontiguousarray(byte.astype(np.uint8).reshape(k // 512, 16, n))


def unpack_weight(words, scales, fmt):
    g, _, n = scales.shape
    words = np.ascontiguousarray(words).reshape(g, 128, n, -1)
    if fmt == "e4m3":
        vals = words.view(ml_dtypes.float8_e4m3fn).astype(np.float64)
    else:
        nib = np.empty((g, 128, n, 4), np.uint8)
        nib[..., 0::2] = words & 0xF
        nib[..., 1::2] = words >> 4
        vals = E2M1[nib]
    vals = vals * np.repeat(np.exp2(scales.astype(np.float64) - 127.0), 8, axis=1)[..., None]
    return vals.transpose(0, 1, 3, 2).reshape(g * 512, n)


def gelu(v):
    return 0.5 * v * (1.0 + np.tanh(np.sqrt(2.0 / np.pi) * (v + 0.044715 * v**3)))


K, T, E, C, H, N = 1536, 512, 4, 256, 512, 128


def by_expert(wq, xq):
    return np.concatenate([wq[e].T @ xq[:, e * C:(e + 1) * C] for e in range(E)], axis=1)


def setup_inputs():
    n = np.random.standard_normal
    s = mx_kscale(K)[:, None]
    u = mx_kscale(H)
    first = np.random.permutation(np.repeat(np.arange(E), T // E))
    second = (first + 1 + np.random.permutation(np.repeat(np.arange(E - 1), -(-T // (E - 1)))[:T])) % E
    while np.bincount(second, minlength=E).max() != T // E:
        load = np.bincount(second, minlength=E); hi, lo = int(load.argmax()), int(load.argmin())
        t = np.flatnonzero((second == hi) & (first != lo))[0]; second[t] = lo
    slot_token = np.empty(E * C, np.int64); pos = np.empty((2, T), np.int64); fill = np.zeros(E, np.int64)
    place = np.stack([np.random.permutation(C) for _ in range(E)])
    for r, deal in enumerate((first, second)):
        for t in np.random.permutation(T):
            e = deal[t]; j = e * C + place[e, fill[e]]; fill[e] += 1; slot_token[j] = t; pos[r, t] = j
    g = np.random.uniform(0.2, 0.8, T)
    x = pack_weight(n((K, T)) * s, "e4m3")
    return {
        "x_words": x[0],
        "x_scales": x[1],
        "w1": (n((E + 1, K, H)) / np.sqrt(K) / s[None] * u[None, None, :]).astype(np.float32),
        "w2": (n((E + 1, H, N)) / np.sqrt(H) / u[None, :, None]).astype(np.float32),
        "gate": np.stack([np.tile(g, (N, 1)), np.tile(1.0 - g, (N, 1))]).astype(np.float32),
        "offs": striped(slot_token),
        "pos1": striped(pos[0]),
        "pos2": striped(pos[1]),
    }


def reference(x_words, x_scales, w1, w2, gate, offs, pos1, pos2):
    idx = unstriped(offs)
    w1q, w2q = mxq(f64(w1), 1, "e4m3"), mxq(f64(w2), 1, "e4m3")
    xs = unpack_weight(x_words, x_scales, "e4m3")
    hs = gelu(w1q[E].T @ xs)
    ys = w2q[E].T @ mxq(hs, 0, "e4m3")
    xq = unpack_weight(x_words, x_scales, "e4m3")[:, idx]
    h = gelu(by_expert(w1q, xq))
    y = by_expert(w2q, mxq(h, 0, "e4m3"))
    return ys + f64(gate[0]) * y[:, unstriped(pos1)] + f64(gate[1]) * y[:, unstriped(pos2)]

@@ -1,0 +1,242 @@
+from contextlib import ExitStack
+
+import concourse.mybir as mybir
+from concourse.masks import make_identity
+
+K, T, E, C, H, N = 1536, 512, 4, 256, 512, 128
+FLOPS = 2 * (E * C + T) * (K * H + H * N)
+
+F32 = mybir.dt.float32
+BF16 = mybir.dt.bfloat16
+I32 = mybir.dt.int32
+U32 = mybir.dt.uint32
+U16 = mybir.dt.uint16
+U8 = mybir.dt.uint8
+FP8X4 = mybir.dt.float8_e4m3fn_x4
+GELU = mybir.ActivationFunctionType.Gelu_apprx_tanh
+MULT = mybir.AluOpType.mult
+ADD = mybir.AluOpType.add
+
+P = 128
+PACK = 4
+PASSES = K // (P * PACK)
+LIST_ROWS = 16
+SPARE = 256
+
+SCALAR_M = [[128, 128, 128], [64, 64, 64], [64, 64, 64], [64, 64, 64], [56, 64, 48]]
+W2_ON_SCALAR = [0, 1, 1, 1, 1]
+Y_ON_VECTOR = [0, 0, 0, 0]
+FINE_FROM = 3
+BF_BUFS = 3
+HOLD = 2
+WARM = 0
+ACC_BUFS = 6
+LAG = [2, 2, 2]
+LAST_LAG = [0, 1]
+Y_CUTS = [0, 512, 1024]
+
+
+def tile_moe_shr_mlp_gelu_kernel(tc, x_words, x_scales, w1, w2, gate, offs, pos1, pos2, out):
+    nc = tc.nc
+    with ExitStack() as ctx:
+        lists = ctx.enter_context(tc.tile_pool(name="lists", bufs=1))
+        keep = ctx.enter_context(tc.tile_pool(name="keep", bufs=1))
+        work = ctx.enter_context(tc.tile_pool(name="work", bufs=4))
+        acc_pool = ctx.enter_context(tc.psum_pool(name="acc", bufs=ACC_BUFS))
+        y_pool = ctx.enter_context(tc.psum_pool(name="ysum", bufs=2))
+
+        offs_sb = lists.tile([P, E * C // LIST_ROWS], U16, name="offs_sb")
+        pos1_sb = lists.tile([P, T // LIST_ROWS], U16, name="pos1_sb")
+        pos2_sb = lists.tile([P, T // LIST_ROWS], U16, name="pos2_sb")
+
+        x_sc = keep.tile([P, T + SPARE], U8, name="x_sc", align_bytes=64)
+        nc.gpsimd.memset(x_sc[:].bitcast(I32), 0)
+        nc.sync.dma_start(offs_sb[:], offs)
+        gate_col = keep.tile([P, 2, 8], F32, name="gate_col")
+        nc.sync.dma_start(gate_col[:, :, 0:PACK], gate[:, 0, :].rearrange("r (p c) -> p r c", c=PACK))
+        x_windows = []
+        for lo, hi in ((0, 1), (1, PASSES)):
+            tile = keep.tile([P, (hi - lo) * T + SPARE], U32, name=f"x_from{lo}", align_bytes=64)
+            nc.vector.memset(tile[:, (hi - lo) * T :].bitcast(I32), 0)
+            nc.sync.dma_start(
+                tile[:, 0 : (hi - lo) * T].rearrange("p (o t) -> p o t", t=T).bitcast(I32),
+                x_words[lo:hi].rearrange("o p t r -> p o (t r)").bitcast(I32),
+            )
+            x_windows.extend(tile[:, o * T : (o + 1) * T + SPARE] for o in range(hi - lo))
+
+        def load_rows(rows, name):
+            raw = keep.tile([P, PACK, rows.shape[1]], F32, name=name, align_bytes=64)
+            nc.sync.dma_start(raw[:], rows.rearrange("(p j) c -> p j c", j=PACK))
+            return raw
+
+        w1_raw = {}
+        w2_raw = {}
+        for e in range(E + 1):
+            for o in range(PASSES):
+                w1_raw[e, o] = load_rows(w1[e, o * P * PACK : (o + 1) * P * PACK, :], f"w1_raw{e}_{o}")
+                if (e, o) == (0, 0):
+                    for q in range(4):
+                        nc.sync.dma_start(
+                            x_sc[32 * q : 32 * q + 4 * PASSES, 0:T].bitcast(I32),
+                            x_scales[:, 4 * q : 4 * q + 4, :].bitcast(I32),
+                        )
+            w2_raw[e] = load_rows(w2[e], f"w2_raw{e}")
+            if e == 1:
+                nc.sync.dma_start(pos1_sb[:], pos1)
+                nc.sync.dma_start(pos2_sb[:], pos2)
+
+        ident = keep.tile([P, P], F32, name="ident")
+        make_identity(nc, ident[:])
+        if WARM:
+            warm = keep.tile([P, 8], F32, name="warm")
+            nc.scalar.activation(warm[:, 0:1], ident[:, 0:1], GELU)
+        gate_sb = []
+        for r in range(2):
+            spread = y_pool.tile([P, PACK, P], F32, name="spread", tag="ysum")
+            for c in range(PACK):
+                nc.tensor.transpose(spread[:, c, :], gate_col[:, r, c : c + 1].to_broadcast([P, P]), ident[:])
+            row = keep.tile([P, T], F32, name=f"gate_sb{r}")
+            nc.scalar.copy(row[:].rearrange("p (n c) -> p n c", c=PACK), spread[:].rearrange("p c n -> p n c"))
+            gate_sb.append(row)
+
+        def quantise(grouped, tag, calls):
+            width = grouped.shape[1] // PACK
+            codes = work.tile([P, width], U32, name=f"{tag}_cd", align_bytes=64, bufs=6)
+            scales = work.tile([P, width], U8, name=f"{tag}_sc", align_bytes=64, bufs=6)
+            step = width // calls
+            for lo in range(0, width, step):
+                cols = slice(lo, lo + step)
+                nc.vector.quantize_mx(codes[:, cols].bitcast(FP8X4), scales[:, cols], grouped[:, PACK * lo : PACK * (lo + step)])
+            return codes, scales
+
+        def cast_w1(e, o):
+            grouped = work.tile([P, PACK * H], BF16, name="w1_bf", align_bytes=64, bufs=BF_BUFS)
+            dst = grouped[:].rearrange("p (t m j) -> p m j t", t=PACK, j=PACK)
+            src = w1_raw[e, o][:].rearrange("p j (m t) -> p m j t", t=PACK)
+            cut = SCALAR_M[e][o]
+            if cut > 0:
+                nc.scalar.copy(dst[:, 0:cut], src[:, 0:cut])
+            if cut < P:
+                nc.vector.tensor_copy(dst[:, cut:P], src[:, cut:P])
+            return grouped
+
+        def cast_w2(e):
+            grouped = work.tile([P, PACK * N], BF16, name="w2_bf", align_bytes=64)
+            copy = nc.scalar.copy if W2_ON_SCALAR[e] else nc.vector.tensor_copy
+            copy(
+                grouped[:].rearrange("p (c i j) -> p c j i", i=4, j=PACK),
+                w2_raw[e][:].rearrange("p j (c i) -> p c j i", i=4),
+            )
+            return grouped
+
+        y_slots = keep.tile([P, E * C], F32, name="y_slots")
+        routed = keep.tile([P, T], F32, name="routed")
+
+        def combine(spent):
+            held = spent[:].bitcast(F32)
+            free = keep.tile([P, 2 * T], F32, name="free")
+            first = held[:, 0:T] if HOLD >= 2 else free[:, 0:T]
+            second = held[:, T : 2 * T] if HOLD >= 1 else free[:, T : 2 * T]
+            nc.vector.tensor_tensor(first, y_slots[:].indirect(pos1_sb[:]), gate_sb[0][:], MULT)
+            nc.vector.tensor_tensor(second, y_slots[:].indirect(pos2_sb[:]), gate_sb[1][:], MULT)
+            nc.vector.tensor_tensor(routed[:], first, second, ADD)
+
+        def mx_pass(e, o):
+            grouped = cast_w1(e, o)
+            return grouped, quantise(grouped[:], "w1", PACK if e >= FINE_FROM and o == PASSES - 1 else 1)
+
+        def first_layer(w1_mx, words, plane, tokens):
+            acc = []
+            for i in range(tokens // P):
+                cols = slice(i * P, (i + 1) * P)
+                bank = acc_pool.tile([P, PACK, P], F32, name="acc")
+                for t in range(PACK):
+                    hidden = slice(t * P, (t + 1) * P)
+                    for o in range(PASSES):
+                        codes, scales = w1_mx[o]
+                        nc.tensor.matmul_mx(
+                            bank[:, t, :],
+                            lhsT=codes[:, hidden].bitcast(FP8X4),
+                            lhsT_scale=scales[:, hidden],
+                            rhs=words[o][:, cols].bitcast(FP8X4),
+                            rhs_scale=plane[4 * o : P, cols],
+                            start=(o == 0),
+                            stop=(o == PASSES - 1),
+                        )
+                acc.append(bank)
+            return acc
+
+        def second_layer(banks, w2_mx, h_bf, ysum):
+            for i, bank in enumerate(banks):
+                nc.scalar.activation(
+                    h_bf[:, i * PACK * P : (i + 1) * PACK * P].rearrange("p (n t) -> p n t", t=PACK),
+                    bank[:].rearrange("p t n -> p n t"),
+                    GELU,
+                )
+            h_codes, h_scales = quantise(h_bf, "h", 1)
+            nc.tensor.matmul_mx(
+                ysum,
+                lhsT=w2_mx[0][:].bitcast(FP8X4),
+                lhsT_scale=w2_mx[1][:],
+                rhs=h_codes[:].bitcast(FP8X4),
+                rhs_scale=h_scales[:],
+                start=True,
+                stop=True,
+            )
+
+        def spent(e, o, tokens):
+            return w1_raw[e, o][:, 0, :].bitcast(BF16)[:, 0 : PACK * tokens]
+
+        y_banks = [y_pool.tile([P, 2 * C], F32, name="y_bank", tag="ysum") for b in range(E // 2)]
+
+        def to_slots(e, first, banks, w2_mx, h_bf):
+            last = first + len(banks) * P
+            bank, lo = divmod(first, 2 * C)
+            second_layer(banks, w2_mx, h_bf, y_banks[bank][:, lo : lo + last - first])
+            if last in Y_CUTS:
+                begin = Y_CUTS[Y_CUTS.index(last) - 1]
+                copy = nc.vector.tensor_copy if Y_ON_VECTOR[e] else nc.scalar.copy
+                copy(y_slots[:, begin:last], y_banks[bank][:, begin - bank * 2 * C : last - bank * 2 * C])
+
+        pair = 2 * C
+        behind = None
+        for e in range(E):
+            if e % 2 == 0:
+                slots = offs_sb[:, e * C // LIST_ROWS : (e * C + pair) // LIST_ROWS]
+                pair_words = []
+                for o in range(PASSES):
+                    got = keep.tile([P, pair], U32, name=f"slot_wd{e}_{o}", align_bytes=64)
+                    nc.vector.tensor_copy(got[:], x_windows[o].indirect(slots))
+                    pair_words.append(got)
+                pair_plane = keep.tile([P, pair], U8, name=f"slot_sc{e}", align_bytes=64)
+                nc.vector.tensor_copy(pair_plane[:], x_sc[:].indirect(slots))
+            mine = slice(e % 2 * C, (e % 2 + 1) * C)
+            w1_mx = []
+            for o in range(PASSES):
+                w1_mx.append(mx_pass(e, o)[1])
+                if behind and o == LAG[e - 1] and o < PASSES - 1:
+                    to_slots(e - 1, (e - 1) * C, *behind, spent(e, o, C))
+            w2_mx = quantise(cast_w2(e)[:], "w2", 1)
+            banks = first_layer(w1_mx, [got[:, mine] for got in pair_words], pair_plane[:, mine], C)
+            if behind and LAG[e - 1] == PASSES - 1:
+                to_slots(e - 1, (e - 1) * C, *behind, spent(e, PASSES - 1, C))
+            behind = (banks, w2_mx)
+
+        w1_mx = []
+        for o in range(PASSES):
+            grouped, mx = mx_pass(E, o)
+            w1_mx.append(mx)
+            for i in range(C // P):
+                if LAST_LAG[i] == o:
+                    to_slots(E - 1, (E - 1) * C + i * P, banks[i : i + 1], w2_mx, spent(E, o, C)[:, i * H : (i + 1) * H])
+        w2_mx = quantise(cast_w2(E)[:], "w2", 1)
+        banks = first_layer(w1_mx, [window[:, 0:T] for window in x_windows], x_sc, T)
+        combine(grouped)
+        for i, bank in enumerate(banks):
+            cols = slice(i * P, (i + 1) * P)
+            h_bf = work.tile([P, PACK * P], BF16, name="h_bf", align_bytes=64)
+            ysum = y_pool.tile([P, P], F32, name="ysum", tag="ysum")
+            second_layer([bank], w2_mx, h_bf[:], ysum[:])
+            result = work.tile([P, P], F32, name="result")
+            nc.vector.tensor_tensor(result[:], ysum[:], routed[:, cols], ADD)
+            nc.sync.dma_start(out[:, cols], result[:])

@@ -230,6 +230,17 @@ def tile_moe_shr_mlp_gelu_kernel(tc, x_words, x_scales, w1, w2, gate, offs, pos1
                 if LAST_LAG[i] == o:
                     to_slots(E - 1, (E - 1) * C + i * P, banks[i : i + 1], w2_mx, spent(E, o, C)[:, i * H : (i + 1) * H])
         w2_mx = quantise(cast_w2(E)[:], "w2", 1)
+        idle = acc_pool.tile([P, T], F32, name="acc")
+        for k in range(3):
+            nc.tensor.matmul_mx(
+                idle[:],
+                lhsT=x_windows[0][:, 0:P].bitcast(FP8X4),
+                lhsT_scale=x_sc[:, 0:P],
+                rhs=w1_mx[1][0][:].bitcast(FP8X4),
+                rhs_scale=w1_mx[1][1][:],
+                start=True,
+                stop=True,
+            )
         banks = first_layer(w1_mx, [window[:, 0:T] for window in x_windows], x_sc, T)
         combine(grouped)
         for i, bank in enumerate(banks):

from contextlib import ExitStack

import concourse.mybir as mybir
from concourse.masks import make_identity

K, T, E, C, H, N = 1536, 512, 4, 256, 512, 128
FLOPS = 2 * (E * C + T) * (K * H + H * N)

F32 = mybir.dt.float32
BF16 = mybir.dt.bfloat16
I32 = mybir.dt.int32
U32 = mybir.dt.uint32
U16 = mybir.dt.uint16
U8 = mybir.dt.uint8
FP8X4 = mybir.dt.float8_e4m3fn_x4
GELU = mybir.ActivationFunctionType.Gelu_apprx_tanh
MULT = mybir.AluOpType.mult
ADD = mybir.AluOpType.add

P = 128
PACK = 4
PASSES = K // (P * PACK)
LIST_ROWS = 16
SPARE = 256

SCALAR_M = [[128, 128, 128], [64, 64, 64], [64, 64, 64], [64, 64, 64], [56, 64, 48]]
W2_ON_SCALAR = [0, 1, 1, 1, 1]
Y_ON_VECTOR = [0, 0, 0, 0]
FINE_FROM = 3
BF_BUFS = 3
HOLD = 2
WARM = 0
ACC_BUFS = 6
LAG = [2, 2, 2]
LAST_LAG = [0, 1]
Y_CUTS = [0, 512, 1024]


def tile_moe_shr_mlp_gelu_kernel(tc, x_words, x_scales, w1, w2, gate, offs, pos1, pos2, out):
    nc = tc.nc
    with ExitStack() as ctx:
        lists = ctx.enter_context(tc.tile_pool(name="lists", bufs=1))
        keep = ctx.enter_context(tc.tile_pool(name="keep", bufs=1))
        work = ctx.enter_context(tc.tile_pool(name="work", bufs=4))
        acc_pool = ctx.enter_context(tc.psum_pool(name="acc", bufs=ACC_BUFS))
        y_pool = ctx.enter_context(tc.psum_pool(name="ysum", bufs=2))

        offs_sb = lists.tile([P, E * C // LIST_ROWS], U16, name="offs_sb")
        pos1_sb = lists.tile([P, T // LIST_ROWS], U16, name="pos1_sb")
        pos2_sb = lists.tile([P, T // LIST_ROWS], U16, name="pos2_sb")

        x_sc = keep.tile([P, T + SPARE], U8, name="x_sc", align_bytes=64)
        nc.gpsimd.memset(x_sc[:].bitcast(I32), 0)
        nc.sync.dma_start(offs_sb[:], offs)
        gate_col = keep.tile([P, 2, 8], F32, name="gate_col")
        nc.sync.dma_start(gate_col[:, :, 0:PACK], gate[:, 0, :].rearrange("r (p c) -> p r c", c=PACK))
        x_windows = []
        for lo, hi in ((0, 1), (1, PASSES)):
            tile = keep.tile([P, (hi - lo) * T + SPARE], U32, name=f"x_from{lo}", align_bytes=64)
            nc.vector.memset(tile[:, (hi - lo) * T :].bitcast(I32), 0)
            nc.sync.dma_start(
                tile[:, 0 : (hi - lo) * T].rearrange("p (o t) -> p o t", t=T).bitcast(I32),
                x_words[lo:hi].rearrange("o p t r -> p o (t r)").bitcast(I32),
            )
            x_windows.extend(tile[:, o * T : (o + 1) * T + SPARE] for o in range(hi - lo))

        def load_rows(rows, name):
            raw = keep.tile([P, PACK, rows.shape[1]], F32, name=name, align_bytes=64)
            nc.sync.dma_start(raw[:], rows.rearrange("(p j) c -> p j c", j=PACK))
            return raw

        w1_raw = {}
        w2_raw = {}
        for e in range(E + 1):
            for o in range(PASSES):
                w1_raw[e, o] = load_rows(w1[e, o * P * PACK : (o + 1) * P * PACK, :], f"w1_raw{e}_{o}")
                if (e, o) == (0, 0):
                    for q in range(4):
                        nc.sync.dma_start(
                            x_sc[32 * q : 32 * q + 4 * PASSES, 0:T].bitcast(I32),
                            x_scales[:, 4 * q : 4 * q + 4, :].bitcast(I32),
                        )
            w2_raw[e] = load_rows(w2[e], f"w2_raw{e}")
            if e == 1:
                nc.sync.dma_start(pos1_sb[:], pos1)
                nc.sync.dma_start(pos2_sb[:], pos2)

        ident = keep.tile([P, P], F32, name="ident")
        make_identity(nc, ident[:])
        if WARM:
            warm = keep.tile([P, 8], F32, name="warm")
            nc.scalar.activation(warm[:, 0:1], ident[:, 0:1], GELU)
        gate_sb = []
        for r in range(2):
            spread = y_pool.tile([P, PACK, P], F32, name="spread", tag="ysum")
            for c in range(PACK):
                nc.tensor.transpose(spread[:, c, :], gate_col[:, r, c : c + 1].to_broadcast([P, P]), ident[:])
            row = keep.tile([P, T], F32, name=f"gate_sb{r}")
            nc.scalar.copy(row[:].rearrange("p (n c) -> p n c", c=PACK), spread[:].rearrange("p c n -> p n c"))
            gate_sb.append(row)

        def quantise(grouped, tag, calls):
            width = grouped.shape[1] // PACK
            codes = work.tile([P, width], U32, name=f"{tag}_cd", align_bytes=64, bufs=6)
            scales = work.tile([P, width], U8, name=f"{tag}_sc", align_bytes=64, bufs=6)
            step = width // calls
            for lo in range(0, width, step):
                cols = slice(lo, lo + step)
                nc.vector.quantize_mx(codes[:, cols].bitcast(FP8X4), scales[:, cols], grouped[:, PACK * lo : PACK * (lo + step)])
            return codes, scales

        def cast_w1(e, o):
            grouped = work.tile([P, PACK * H], BF16, name="w1_bf", align_bytes=64, bufs=BF_BUFS)
            dst = grouped[:].rearrange("p (t m j) -> p m j t", t=PACK, j=PACK)
            src = w1_raw[e, o][:].rearrange("p j (m t) -> p m j t", t=PACK)
            cut = SCALAR_M[e][o]
            if cut > 0:
                nc.scalar.copy(dst[:, 0:cut], src[:, 0:cut])
            if cut < P:
                nc.vector.tensor_copy(dst[:, cut:P], src[:, cut:P])
            return grouped

        def cast_w2(e):
            grouped = work.tile([P, PACK * N], BF16, name="w2_bf", align_bytes=64)
            copy = nc.scalar.copy if W2_ON_SCALAR[e] else nc.vector.tensor_copy
            copy(
                grouped[:].rearrange("p (c i j) -> p c j i", i=4, j=PACK),
                w2_raw[e][:].rearrange("p j (c i) -> p c j i", i=4),
            )
            return grouped

        y_slots = keep.tile([P, E * C], F32, name="y_slots")
        routed = keep.tile([P, T], F32, name="routed")

        def combine(spent):
            held = spent[:].bitcast(F32)
            free = keep.tile([P, 2 * T], F32, name="free")
            first = held[:, 0:T] if HOLD >= 2 else free[:, 0:T]
            second = held[:, T : 2 * T] if HOLD >= 1 else free[:, T : 2 * T]
            nc.vector.tensor_tensor(first, y_slots[:].indirect(pos1_sb[:]), gate_sb[0][:], MULT)
            nc.vector.tensor_tensor(second, y_slots[:].indirect(pos2_sb[:]), gate_sb[1][:], MULT)
            nc.vector.tensor_tensor(routed[:], first, second, ADD)

        def mx_pass(e, o):
            grouped = cast_w1(e, o)
            return grouped, quantise(grouped[:], "w1", PACK if e >= FINE_FROM and o == PASSES - 1 else 1)

        def first_layer(w1_mx, words, plane, tokens):
            acc = []
            for i in range(tokens // P):
                cols = slice(i * P, (i + 1) * P)
                bank = acc_pool.tile([P, PACK, P], F32, name="acc")
                for t in range(PACK):
                    hidden = slice(t * P, (t + 1) * P)
                    for o in range(PASSES):
                        codes, scales = w1_mx[o]
                        nc.tensor.matmul_mx(
                            bank[:, t, :],
                            lhsT=codes[:, hidden].bitcast(FP8X4),
                            lhsT_scale=scales[:, hidden],
                            rhs=words[o][:, cols].bitcast(FP8X4),
                            rhs_scale=plane[4 * o : P, cols],
                            start=(o == 0),
                            stop=(o == PASSES - 1),
                        )
                acc.append(bank)
            return acc

        def second_layer(banks, w2_mx, h_bf, ysum):
            for i, bank in enumerate(banks):
                nc.scalar.activation(
                    h_bf[:, i * PACK * P : (i + 1) * PACK * P].rearrange("p (n t) -> p n t", t=PACK),
                    bank[:].rearrange("p t n -> p n t"),
                    GELU,
                )
            h_codes, h_scales = quantise(h_bf, "h", 1)
            nc.tensor.matmul_mx(
                ysum,
                lhsT=w2_mx[0][:].bitcast(FP8X4),
                lhsT_scale=w2_mx[1][:],
                rhs=h_codes[:].bitcast(FP8X4),
                rhs_scale=h_scales[:],
                start=True,
                stop=True,
            )

        def spent(e, o, tokens):
            return w1_raw[e, o][:, 0, :].bitcast(BF16)[:, 0 : PACK * tokens]

        y_banks = [y_pool.tile([P, 2 * C], F32, name="y_bank", tag="ysum") for b in range(E // 2)]

        def to_slots(e, first, banks, w2_mx, h_bf):
            last = first + len(banks) * P
            bank, lo = divmod(first, 2 * C)
            second_layer(banks, w2_mx, h_bf, y_banks[bank][:, lo : lo + last - first])
            if last in Y_CUTS:
                begin = Y_CUTS[Y_CUTS.index(last) - 1]
                copy = nc.vector.tensor_copy if Y_ON_VECTOR[e] else nc.scalar.copy
                copy(y_slots[:, begin:last], y_banks[bank][:, begin - bank * 2 * C : last - bank * 2 * C])

        pair = 2 * C
        behind = None
        for e in range(E):
            if e % 2 == 0:
                slots = offs_sb[:, e * C // LIST_ROWS : (e * C + pair) // LIST_ROWS]
                pair_words = []
                for o in range(PASSES):
                    got = keep.tile([P, pair], U32, name=f"slot_wd{e}_{o}", align_bytes=64)
                    nc.vector.tensor_copy(got[:], x_windows[o].indirect(slots))
                    pair_words.append(got)
                pair_plane = keep.tile([P, pair], U8, name=f"slot_sc{e}", align_bytes=64)
                nc.vector.tensor_copy(pair_plane[:], x_sc[:].indirect(slots))
            mine = slice(e % 2 * C, (e % 2 + 1) * C)
            w1_mx = []
            for o in range(PASSES):
                w1_mx.append(mx_pass(e, o)[1])
                if behind and o == LAG[e - 1] and o < PASSES - 1:
                    to_slots(e - 1, (e - 1) * C, *behind, spent(e, o, C))
            w2_mx = quantise(cast_w2(e)[:], "w2", 1)
            banks = first_layer(w1_mx, [got[:, mine] for got in pair_words], pair_plane[:, mine], C)
            if behind and LAG[e - 1] == PASSES - 1:
                to_slots(e - 1, (e - 1) * C, *behind, spent(e, PASSES - 1, C))
            behind = (banks, w2_mx)

        w1_mx = []
        for o in range(PASSES):
            grouped, mx = mx_pass(E, o)
            w1_mx.append(mx)
            for i in range(C // P):
                if LAST_LAG[i] == o:
                    to_slots(E - 1, (E - 1) * C + i * P, banks[i : i + 1], w2_mx, spent(E, o, C)[:, i * H : (i + 1) * H])
        w2_mx = quantise(cast_w2(E)[:], "w2", 1)
        idle = acc_pool.tile([P, T], F32, name="acc")
        for k in range(3):
            nc.tensor.matmul_mx(
                idle[:],
                lhsT=x_windows[0][:, 0:P].bitcast(FP8X4),
                lhsT_scale=x_sc[:, 0:P],
                rhs=w1_mx[1][0][:].bitcast(FP8X4),
                rhs_scale=w1_mx[1][1][:],
                start=True,
                stop=True,
            )
        banks = first_layer(w1_mx, [window[:, 0:T] for window in x_windows], x_sc, T)
        combine(grouped)
        for i, bank in enumerate(banks):
            cols = slice(i * P, (i + 1) * P)
            h_bf = work.tile([P, PACK * P], BF16, name="h_bf", align_bytes=64)
            ysum = y_pool.tile([P, P], F32, name="ysum", tag="ysum")
            second_layer([bank], w2_mx, h_bf[:], ysum[:])
            result = work.tile([P, P], F32, name="result")
            nc.vector.tensor_tensor(result[:], ysum[:], routed[:, cols], ADD)
            nc.sync.dma_start(out[:, cols], result[:])
